import numpy as np
import ml_dtypes


def mxq(x, axis, fmt="e4m3"):
    dtype, down = {"e4m3": (ml_dtypes.float8_e4m3fn, 7), "e5m2": (ml_dtypes.float8_e5m2, 14)}[fmt]
    v = np.moveaxis(np.asarray(x, np.float32).astype(ml_dtypes.bfloat16).astype(np.float64), axis, -1)
    blocks = v.reshape(v.shape[:-1] + (-1, 32))
    amax = np.abs(blocks).max(-1, keepdims=True)
    byte = np.maximum(np.where(amax > 0, np.frexp(amax)[1] - 1 + 127, 0) - down, 1)
    scale = np.exp2(byte - 127.0)
    codes = (blocks / scale).astype(np.float32).astype(dtype).astype(np.float64)
    return np.moveaxis((codes * scale).reshape(v.shape), -1, axis)


WIDE = False


def mx_kscale(k):
    if not WIDE:
        return np.ones(k)
    levels = np.array([10, -10, 5, -5, 0])
    if k % 512:
        return np.exp2(np.random.permutation(np.resize(levels, k // 32))).repeat(32)
    a = np.empty((k // 512, 16))
    for p in range(k // 512):
        a[p, :8] = np.random.permutation(np.resize(levels, 8))
        for g in range(8):
            far = levels[np.abs(levels - a[p, g]) >= 10]
            a[p, g + 8] = far[np.random.randint(len(far))]
    return np.exp2(a.ravel()).repeat(32)


def f64(x):
    return np.asarray(x).astype(np.float64)


E2M1 = np.array([0.0, 0.5, 1.0, 1.5, 2.0, 3.0, 4.0, 6.0, -0.0, -0.5, -1.0, -1.5, -2.0, -3.0, -4.0, -6.0])


def pack_weight(w, fmt):
    k, n = w.shape
    w = f64(np.asarray(w, np.float32).astype(ml_dtypes.bfloat16)).reshape(k // 32, 32, n)
    amax = np.abs(w).max(1)
    if fmt == "e4m3":
        byte = np.frexp(amax)[1] - 1 + 127 - 7
    else:
        mant, ex = np.frexp(amax / 6.0)
        byte = np.where(mant > 0.5, ex, ex - 1) + 127
    byte = np.clip(np.where(amax > 0, byte, 1), 1, 254)
    scaled = (w * np.exp2(127.0 - byte)[:, None, :]).reshape(k, n).astype(np.float32)
    by_word = np.ascontiguousarray(scaled.reshape(k // 512, 128, 4, n).transpose(0, 1, 3, 2))
    if fmt == "e4m3":
        words = by_word.astype(ml_dtypes.float8_e4m3fn).view(np.uint8)
    else:
        c = by_word.astype(ml_dtypes.float4_e2m1fn).view(np.uint8) & 0xF
        words = (c[..., 0::2] | (c[..., 1::2] << 4)).reshape(k // 512, 128, 2 * n)
    return np.ascontiguousarray(words), np.ascontiguousarray(byte.astype(np.uint8).reshape(k // 512, 16, n))


def unpack_weight(words, scales, fmt):
    g, _, n = scales.shape
    words = np.ascontiguousarray(words).reshape(g, 128, n, -1)
    if fmt == "e4m3":
        vals = words.view(ml_dtypes.float8_e4m3fn).astype(np.float64)
    else:
        nib = np.empty((g, 128, n, 4), np.uint8)
        nib[..., 0::2] = words & 0xF
        nib[..., 1::2] = words >> 4
        vals = E2M1[nib]
    vals = vals * np.repeat(np.exp2(scales.astype(np.float64) - 127.0), 8, axis=1)[..., None]
    return vals.transpose(0, 1, 3, 2).reshape(g * 512, n)


O, K, M, T = 1024, 3072, 512, 1024


def setup_inputs():
    n = np.random.standard_normal
    s = mx_kscale(K)[:, None]
    x = n((K, T)); x[:O] *= 6.0
    w = n((K, M)) / np.sqrt(K) / s; w[:O] /= 2.0
    p_x4 = pack_weight(x[O:] * s[O:], "e2m1")
    p_w4 = pack_weight(w[O:], "e2m1")
    return {
        "x8": (x[:O] * s[:O]).astype(np.float32),
        "w8": (w[:O]).astype(np.float32),
        "x4_words": p_x4[0],
        "x4_scales": p_x4[1],
        "w4_words": p_w4[0],
        "w4_scales": p_w4[1],
    }


def reference(x8, w8, x4_words, x4_scales, w4_words, w4_scales):
    x8_ = mxq(f64(x8), 0, "e4m3")
    w8_ = mxq(f64(w8), 0, "e4m3")
    x4_ = unpack_weight(x4_words, x4_scales, "e2m1")
    w4_ = unpack_weight(w4_words, w4_scales, "e2m1")
    y = x8_.T @ w8_ + x4_.T @ w4_
    return y

@@ -1,0 +1,173 @@
+from contextlib import ExitStack
+
+import concourse.mybir as mybir
+
+K8, K4, M, T = 1024, 2048, 512, 1024
+FLOPS = 2 * (K8 + K4) * M * T
+
+F32 = mybir.dt.float32
+BF16 = mybir.dt.bfloat16
+I32 = mybir.dt.int32
+U32 = mybir.dt.uint32
+U8 = mybir.dt.uint8
+FP8X4 = mybir.dt.float8_e4m3fn_x4
+FP4X4 = mybir.dt.float4_e2m1fn_x4
+
+P = 128
+PACK = 4
+A8 = K8 // 512
+A4 = K4 // 512
+TILES = T // P
+
+
+def tile_mix_atom_tm_none_kernel(tc, x8, w8, x4_words, x4_scales, w4_words, w4_scales, out):
+    nc = tc.nc
+    x8_rows = x8.rearrange("(a p j) t -> a p j t", p=P, j=PACK)
+    w8_rows = w8.rearrange("(a p j) n -> a p j n", p=P, j=PACK)
+    x4_rows = x4_words.rearrange("a p c -> p a c")
+    w4_rows = w4_words.rearrange("a p c -> p a c")
+    x4_srows = x4_scales.rearrange("a (q r) t -> r q a t", r=4)
+    w4_srows = w4_scales.rearrange("a (q r) n -> r q a n", r=4)
+    out_rows = out.rearrange("(i p) n -> p i n", p=P)
+
+    with ExitStack() as ctx:
+        keep = ctx.enter_context(tc.tile_pool(name="keep", bufs=1))
+        psum = ctx.enter_context(tc.psum_pool(name="psum", bufs=1))
+
+        x4_sb = keep.tile([P, A4, 2 * T], U8, name="x4_sb", align_bytes=64)
+        w4_sb = keep.tile([P, A4, 2 * M], U8, name="w4_sb", align_bytes=64)
+        x4_sc = keep.tile([P, A4, T], U8, name="x4_sc", align_bytes=64)
+        w4_sc = keep.tile([P, A4, M], U8, name="w4_sc", align_bytes=64)
+        x8_codes = keep.tile([P, A8, T], U32, name="x8_codes", align_bytes=64)
+        x8_sc = keep.tile([P, A8, T], U8, name="x8_sc", align_bytes=64)
+        w8_codes = keep.tile([P, A8, M], U32, name="w8_codes", align_bytes=64)
+        w8_sc = keep.tile([P, A8, M], U8, name="w8_sc", align_bytes=64)
+        o_sb = keep.tile([P, TILES, M], F32, name="o_sb", align_bytes=64)
+        warm = keep.tile([P, 8], F32, name="warm")
+        warm_out = keep.tile([P, 8], F32, name="warm_out")
+        banks = [psum.tile([P, M], F32, name=f"bank{i}") for i in range(TILES)]
+
+        pieces = {
+            "w0": (w8_rows, 0, 0, 512),
+            "w1": (w8_rows, 1, 0, 512),
+            "x0": (x8_rows, 0, 0, 512),
+            "x1": (x8_rows, 1, 0, 512),
+            "x2": (x8_rows, 0, 512, 512),
+            "x3": (x8_rows, 1, 512, 256),
+            "x4": (x8_rows, 1, 768, 256),
+        }
+        raw = {}
+        grouped = {}
+        for key, (rows, a, c0, width) in pieces.items():
+            raw[key] = keep.tile([P, PACK, width], F32, name=f"raw_{key}", align_bytes=64)
+            grouped[key] = keep.tile([P, width, PACK], BF16, name=f"grouped_{key}", align_bytes=64)
+
+        def load(key):
+            rows, a, c0, width = pieces[key]
+            nc.sync.dma_start(out=raw[key][:], in_=rows[a][:, :, c0 : c0 + width])
+
+        def cast(copy, key, lo, hi):
+            copy(out=grouped[key][:, lo:hi, :], in_=raw[key][:, :, lo:hi].rearrange("p j w -> p w j"))
+
+        def quantize(key, lo, hi):
+            rows, a, c0, width = pieces[key]
+            codes, scales = (w8_codes, w8_sc) if key[0] == "w" else (x8_codes, x8_sc)
+            nc.vector.quantize_mx(
+                out=codes[:, a, c0 + lo : c0 + hi].bitcast(FP8X4),
+                scales=scales[:, a, c0 + lo : c0 + hi],
+                in_=grouped[key][:, lo:hi, :].rearrange("p w j -> p (w j)"),
+            )
+
+        def pass4(i, a):
+            t = slice(P * i, P * (i + 1))
+            nc.tensor.matmul_mx(
+                out=banks[i][:],
+                lhsT=x4_sb[:, a, 2 * P * i : 2 * P * (i + 1)].bitcast(FP4X4),
+                lhsT_scale=x4_sc[:, a, t],
+                rhs=w4_sb[:, a, :].bitcast(FP4X4),
+                rhs_scale=w4_sc[:, a, :],
+                start=(a == 0),
+                stop=False,
+            )
+
+        def pass8(i, a):
+            t = slice(P * i, P * (i + 1))
+            nc.tensor.matmul_mx(
+                out=banks[i][:],
+                lhsT=x8_codes[:, a, t].bitcast(FP8X4),
+                lhsT_scale=x8_sc[:, a, t],
+                rhs=w8_codes[:, a, :].bitcast(FP8X4),
+                rhs_scale=w8_sc[:, a, :],
+                start=False,
+                stop=(a == A8 - 1),
+            )
+
+        def drain(copy, i):
+            copy(out=o_sb[:, i, :], in_=banks[i][:])
+
+        def store(i0, i1):
+            nc.sync.dma_start(out=out_rows[:, i0:i1, :], in_=o_sb[:, i0:i1, :])
+
+        v, s = nc.vector.tensor_copy, nc.scalar.copy
+
+        with tc.manual_schedule():
+            nc.sync.dma_start(out=w4_sb[:].bitcast(I32), in_=w4_rows.bitcast(I32))
+            for a in (0, 2):
+                nc.sync.dma_start(out=x4_sb[:, a : a + 2, :].bitcast(I32), in_=x4_rows[:, a : a + 2, :].bitcast(I32))
+            nc.gpsimd.memset(w4_sc[:].bitcast(I32), 0)
+            nc.vector.memset(x4_sc[:].bitcast(I32), 0)
+            nc.vector.memset(warm[:], 0.0)
+            for r in range(4):
+                nc.scalar.dma_start(out=x4_sc[r:P:32, :, :].bitcast(I32), in_=x4_srows[r].bitcast(I32))
+                nc.gpsimd.dma_start(out=w4_sc[r:P:32, :, :].bitcast(I32), in_=w4_srows[r].bitcast(I32))
+            s(out=warm_out[:], in_=warm[:])
+            for key in pieces:
+                load(key)
+
+            for i0 in (0, 4):
+                for a in range(A4):
+                    for i in range(i0, i0 + 4):
+                        pass4(i, a)
+
+            def big(key):
+                cast(v, key, 0, 128)
+                cast(v, key, 128, 256)
+                cast(s, key, 256, 384)
+                cast(s, key, 384, 512)
+                quantize(key, 0, 128)
+                quantize(key, 128, 256)
+                quantize(key, 256, 512)
+
+            def small(key):
+                cast(v, key, 0, 128)
+                cast(s, key, 128, 256)
+                quantize(key, 0, 128)
+                quantize(key, 128, 256)
+
+            for key in ("w0", "w1", "x0", "x1"):
+                big(key)
+            for i in range(4):
+                pass8(i, 0)
+                pass8(i, 1)
+            big("x2")
+            drain(s, 0)
+            drain(s, 1)
+            store(0, 2)
+            for i in range(4, 8):
+                pass8(i, 0)
+            small("x3")
+            drain(s, 2)
+            drain(s, 3)
+            store(2, 4)
+            pass8(4, 1)
+            pass8(5, 1)
+            small("x4")
+            drain(v, 4)
+            drain(s, 5)
+            store(4, 6)
+            pass8(6, 1)
+            pass8(7, 1)
+            drain(v, 6)
+            store(6, 7)
+            drain(s, 7)
+            store(7, 8)

@@ -112,14 +112,14 @@ def tile_mix_atom_tm_none_kernel(tc, x8, w8, x4_words, x4_scales, w4_words, w4_s
 
         with tc.manual_schedule():
             nc.sync.dma_start(out=w4_sb[:].bitcast(I32), in_=w4_rows.bitcast(I32))
-            for a in (0, 2):
-                nc.sync.dma_start(out=x4_sb[:, a : a + 2, :].bitcast(I32), in_=x4_rows[:, a : a + 2, :].bitcast(I32))
             nc.gpsimd.memset(w4_sc[:].bitcast(I32), 0)
             nc.vector.memset(x4_sc[:].bitcast(I32), 0)
             nc.vector.memset(warm[:], 0.0)
             for r in range(4):
-                nc.scalar.dma_start(out=x4_sc[r:P:32, :, :].bitcast(I32), in_=x4_srows[r].bitcast(I32))
+                nc.sync.dma_start(out=x4_sc[r:P:32, :, :].bitcast(I32), in_=x4_srows[r].bitcast(I32))
                 nc.gpsimd.dma_start(out=w4_sc[r:P:32, :, :].bitcast(I32), in_=w4_srows[r].bitcast(I32))
+            for a in (0, 2):
+                nc.sync.dma_start(out=x4_sb[:, a : a + 2, :].bitcast(I32), in_=x4_rows[:, a : a + 2, :].bitcast(I32))
             s(out=warm_out[:], in_=warm[:])
             for key in pieces:
                 load(key)

@@ -111,60 +111,67 @@ def tile_mix_atom_tm_none_kernel(tc, x8, w8, x4_words, x4_scales, w4_words, w4_s
         v, s = nc.vector.tensor_copy, nc.scalar.copy
 
         with tc.manual_schedule():
-            nc.sync.dma_start(out=w4_sb[:].bitcast(I32), in_=w4_rows.bitcast(I32))
             nc.gpsimd.memset(w4_sc[:].bitcast(I32), 0)
             nc.vector.memset(x4_sc[:].bitcast(I32), 0)
             nc.vector.memset(warm[:], 0.0)
-            for r in range(4):
-                nc.sync.dma_start(out=x4_sc[r:P:32, :, :].bitcast(I32), in_=x4_srows[r].bitcast(I32))
-                nc.gpsimd.dma_start(out=w4_sc[r:P:32, :, :].bitcast(I32), in_=w4_srows[r].bitcast(I32))
-            for a in (0, 2):
-                nc.sync.dma_start(out=x4_sb[:, a : a + 2, :].bitcast(I32), in_=x4_rows[:, a : a + 2, :].bitcast(I32))
             s(out=warm_out[:], in_=warm[:])
-            for key in pieces:
+
+            def load_scales(plane, rows, r):
+                nc.sync.dma_start(out=plane[r:P:32, :, :].bitcast(I32), in_=rows[r].bitcast(I32))
+
+            def load_x4(a):
+                nc.sync.dma_start(out=x4_sb[:, a : a + 2, :].bitcast(I32), in_=x4_rows[:, a : a + 2, :].bitcast(I32))
+
+            for r in range(3):
+                load_scales(w4_sc, w4_srows, r)
+            nc.sync.dma_start(out=w4_sb[:].bitcast(I32), in_=w4_rows.bitcast(I32))
+            load_x4(0)
+            load_scales(w4_sc, w4_srows, 3)
+            for r in range(4):
+                load_scales(x4_sc, x4_srows, r)
+            load("w0")
+            load_x4(2)
+            for key in ("w1", "x0", "x1", "x2", "x3", "x4"):
                 load(key)
 
-            for i0 in (0, 4):
-                for a in range(A4):
-                    for i in range(i0, i0 + 4):
-                        pass4(i, a)
-
             def big(key):
-                cast(v, key, 0, 128)
-                cast(v, key, 128, 256)
-                cast(s, key, 256, 384)
-                cast(s, key, 384, 512)
-                quantize(key, 0, 128)
-                quantize(key, 128, 256)
+                cast(v, key, 0, 256)
+                cast(s, key, 256, 512)
+                quantize(key, 0, 256)
                 quantize(key, 256, 512)
 
             def small(key):
                 cast(v, key, 0, 128)
-                cast(s, key, 128, 256)
+                cast(v, key, 128, 256)
                 quantize(key, 0, 128)
                 quantize(key, 128, 256)
 
+            for a0 in (0, 2):
+                for i in range(TILES):
+                    pass4(i, a0)
+                    pass4(i, a0 + 1)
             for key in ("w0", "w1", "x0", "x1"):
                 big(key)
-            for i in range(4):
-                pass8(i, 0)
-                pass8(i, 1)
+            for a in range(A8):
+                for i in range(4):
+                    pass8(i, a)
             big("x2")
             drain(s, 0)
             drain(s, 1)
             store(0, 2)
-            for i in range(4, 8):
-                pass8(i, 0)
-            small("x3")
             drain(s, 2)
             drain(s, 3)
             store(2, 4)
+            for i in range(4, 8):
+                pass8(i, 0)
+            small("x3")
             pass8(4, 1)
             pass8(5, 1)
             small("x4")
             drain(v, 4)
+            store(4, 5)
             drain(s, 5)
-            store(4, 6)
+            store(5, 6)
             pass8(6, 1)
             pass8(7, 1)
             drain(v, 6)

@@ -67,7 +67,10 @@ def tile_mix_atom_tm_none_kernel(tc, x8, w8, x4_words, x4_scales, w4_words, w4_s
             nc.sync.dma_start(out=raw[key][:], in_=rows[a][:, :, c0 : c0 + width])
 
         def cast(copy, key, lo, hi):
-            copy(out=grouped[key][:, lo:hi, :], in_=raw[key][:, :, lo:hi].rearrange("p j w -> p w j"))
+            copy(
+                out=grouped[key][:, lo:hi, :].rearrange("p (c i) j -> p c j i", i=4),
+                in_=raw[key][:, :, lo:hi].rearrange("p j (c i) -> p c j i", i=4),
+            )
 
         def quantize(key, lo, hi):
             rows, a, c0, width = pieces[key]
@@ -122,11 +125,10 @@ def tile_mix_atom_tm_none_kernel(tc, x8, w8, x4_words, x4_scales, w4_words, w4_s
             def load_x4(a):
                 nc.sync.dma_start(out=x4_sb[:, a : a + 2, :].bitcast(I32), in_=x4_rows[:, a : a + 2, :].bitcast(I32))
 
-            for r in range(3):
-                load_scales(w4_sc, w4_srows, r)
             nc.sync.dma_start(out=w4_sb[:].bitcast(I32), in_=w4_rows.bitcast(I32))
             load_x4(0)
-            load_scales(w4_sc, w4_srows, 3)
+            for r in range(4):
+                load_scales(w4_sc, w4_srows, r)
             for r in range(4):
                 load_scales(x4_sc, x4_srows, r)
             load("w0")
@@ -140,41 +142,49 @@ def tile_mix_atom_tm_none_kernel(tc, x8, w8, x4_words, x4_scales, w4_words, w4_s
                 quantize(key, 0, 256)
                 quantize(key, 256, 512)
 
-            def small(key):
-                cast(v, key, 0, 128)
-                cast(v, key, 128, 256)
-                quantize(key, 0, 128)
-                quantize(key, 128, 256)
-
-            for a0 in (0, 2):
-                for i in range(TILES):
-                    pass4(i, a0)
-                    pass4(i, a0 + 1)
+            for i in range(TILES):
+                pass4(i, 0)
+                pass4(i, 1)
+            for i in range(6):
+                pass4(i, 2)
+                pass4(i, 3)
             for key in ("w0", "w1", "x0", "x1"):
                 big(key)
             for a in range(A8):
                 for i in range(4):
                     pass8(i, a)
-            big("x2")
+            for i in range(6, TILES):
+                pass4(i, 2)
+                pass4(i, 3)
             drain(s, 0)
-            drain(s, 1)
+            drain(v, 1)
             store(0, 2)
+            cast(v, "x2", 0, 256)
+            cast(s, "x2", 256, 512)
+            quantize("x2", 0, 256)
             drain(s, 2)
             drain(s, 3)
             store(2, 4)
+            cast(v, "x3", 0, 128)
+            quantize("x2", 256, 512)
             for i in range(4, 8):
                 pass8(i, 0)
-            small("x3")
+            quantize("x3", 0, 128)
             pass8(4, 1)
+            cast(v, "x3", 128, 256)
+            quantize("x3", 128, 256)
             pass8(5, 1)
-            small("x4")
+            cast(s, "x4", 0, 128)
+            cast(s, "x4", 128, 256)
             drain(v, 4)
             store(4, 5)
-            drain(s, 5)
-            store(5, 6)
+            quantize("x4", 0, 128)
             pass8(6, 1)
+            drain(v, 5)
+            store(5, 6)
+            quantize("x4", 128, 256)
             pass8(7, 1)
-            drain(v, 6)
+            drain(s, 6)
             store(6, 7)
             drain(s, 7)
             store(7, 8)

from contextlib import ExitStack

import concourse.mybir as mybir

K8, K4, M, T = 1024, 2048, 512, 1024
FLOPS = 2 * (K8 + K4) * M * T

F32 = mybir.dt.float32
BF16 = mybir.dt.bfloat16
I32 = mybir.dt.int32
U32 = mybir.dt.uint32
U8 = mybir.dt.uint8
FP8X4 = mybir.dt.float8_e4m3fn_x4
FP4X4 = mybir.dt.float4_e2m1fn_x4

P = 128
PACK = 4
A8 = K8 // 512
A4 = K4 // 512
TILES = T // P


def tile_mix_atom_tm_none_kernel(tc, x8, w8, x4_words, x4_scales, w4_words, w4_scales, out):
    nc = tc.nc
    x8_rows = x8.rearrange("(a p j) t -> a p j t", p=P, j=PACK)
    w8_rows = w8.rearrange("(a p j) n -> a p j n", p=P, j=PACK)
    x4_rows = x4_words.rearrange("a p c -> p a c")
    w4_rows = w4_words.rearrange("a p c -> p a c")
    x4_srows = x4_scales.rearrange("a (q r) t -> r q a t", r=4)
    w4_srows = w4_scales.rearrange("a (q r) n -> r q a n", r=4)
    out_rows = out.rearrange("(i p) n -> p i n", p=P)

    with ExitStack() as ctx:
        keep = ctx.enter_context(tc.tile_pool(name="keep", bufs=1))
        psum = ctx.enter_context(tc.psum_pool(name="psum", bufs=1))

        x4_sb = keep.tile([P, A4, 2 * T], U8, name="x4_sb", align_bytes=64)
        w4_sb = keep.tile([P, A4, 2 * M], U8, name="w4_sb", align_bytes=64)
        x4_sc = keep.tile([P, A4, T], U8, name="x4_sc", align_bytes=64)
        w4_sc = keep.tile([P, A4, M], U8, name="w4_sc", align_bytes=64)
        x8_codes = keep.tile([P, A8, T], U32, name="x8_codes", align_bytes=64)
        x8_sc = keep.tile([P, A8, T], U8, name="x8_sc", align_bytes=64)
        w8_codes = keep.tile([P, A8, M], U32, name="w8_codes", align_bytes=64)
        w8_sc = keep.tile([P, A8, M], U8, name="w8_sc", align_bytes=64)
        o_sb = keep.tile([P, TILES, M], F32, name="o_sb", align_bytes=64)
        warm = keep.tile([P, 8], F32, name="warm")
        warm_out = keep.tile([P, 8], F32, name="warm_out")
        banks = [psum.tile([P, M], F32, name=f"bank{i}") for i in range(TILES)]

        pieces = {
            "w0": (w8_rows, 0, 0, 512),
            "w1": (w8_rows, 1, 0, 512),
            "x0": (x8_rows, 0, 0, 512),
            "x1": (x8_rows, 1, 0, 512),
            "x2": (x8_rows, 0, 512, 512),
            "x3": (x8_rows, 1, 512, 256),
            "x4": (x8_rows, 1, 768, 256),
        }
        raw = {}
        grouped = {}
        for key, (rows, a, c0, width) in pieces.items():
            raw[key] = keep.tile([P, PACK, width], F32, name=f"raw_{key}", align_bytes=64)
            grouped[key] = keep.tile([P, width, PACK], BF16, name=f"grouped_{key}", align_bytes=64)

        def load(key):
            rows, a, c0, width = pieces[key]
            nc.sync.dma_start(out=raw[key][:], in_=rows[a][:, :, c0 : c0 + width])

        def cast(copy, key, lo, hi):
            copy(
                out=grouped[key][:, lo:hi, :].rearrange("p (c i) j -> p c j i", i=4),
                in_=raw[key][:, :, lo:hi].rearrange("p j (c i) -> p c j i", i=4),
            )

        def quantize(key, lo, hi):
            rows, a, c0, width = pieces[key]
            codes, scales = (w8_codes, w8_sc) if key[0] == "w" else (x8_codes, x8_sc)
            nc.vector.quantize_mx(
                out=codes[:, a, c0 + lo : c0 + hi].bitcast(FP8X4),
                scales=scales[:, a, c0 + lo : c0 + hi],
                in_=grouped[key][:, lo:hi, :].rearrange("p w j -> p (w j)"),
            )

        def pass4(i, a):
            t = slice(P * i, P * (i + 1))
            nc.tensor.matmul_mx(
                out=banks[i][:],
                lhsT=x4_sb[:, a, 2 * P * i : 2 * P * (i + 1)].bitcast(FP4X4),
                lhsT_scale=x4_sc[:, a, t],
                rhs=w4_sb[:, a, :].bitcast(FP4X4),
                rhs_scale=w4_sc[:, a, :],
                start=(a == 0),
                stop=False,
            )

        def pass8(i, a):
            t = slice(P * i, P * (i + 1))
            nc.tensor.matmul_mx(
                out=banks[i][:],
                lhsT=x8_codes[:, a, t].bitcast(FP8X4),
                lhsT_scale=x8_sc[:, a, t],
                rhs=w8_codes[:, a, :].bitcast(FP8X4),
                rhs_scale=w8_sc[:, a, :],
                start=False,
                stop=(a == A8 - 1),
            )

        def drain(copy, i):
            copy(out=o_sb[:, i, :], in_=banks[i][:])

        def store(i0, i1):
            nc.sync.dma_start(out=out_rows[:, i0:i1, :], in_=o_sb[:, i0:i1, :])

        v, s = nc.vector.tensor_copy, nc.scalar.copy

        with tc.manual_schedule():
            nc.gpsimd.memset(w4_sc[:].bitcast(I32), 0)
            nc.vector.memset(x4_sc[:].bitcast(I32), 0)
            nc.vector.memset(warm[:], 0.0)
            s(out=warm_out[:], in_=warm[:])

            def load_scales(plane, rows, r):
                nc.sync.dma_start(out=plane[r:P:32, :, :].bitcast(I32), in_=rows[r].bitcast(I32))

            def load_x4(a):
                nc.sync.dma_start(out=x4_sb[:, a : a + 2, :].bitcast(I32), in_=x4_rows[:, a : a + 2, :].bitcast(I32))

            nc.sync.dma_start(out=w4_sb[:].bitcast(I32), in_=w4_rows.bitcast(I32))
            load_x4(0)
            for r in range(4):
                load_scales(w4_sc, w4_srows, r)
            for r in range(4):
                load_scales(x4_sc, x4_srows, r)
            load("w0")
            load_x4(2)
            for key in ("w1", "x0", "x1", "x2", "x3", "x4"):
                load(key)

            def big(key):
                cast(v, key, 0, 256)
                cast(s, key, 256, 512)
                quantize(key, 0, 256)
                quantize(key, 256, 512)

            for i in range(TILES):
                pass4(i, 0)
                pass4(i, 1)
            for i in range(6):
                pass4(i, 2)
                pass4(i, 3)
            for key in ("w0", "w1", "x0", "x1"):
                big(key)
            for a in range(A8):
                for i in range(4):
                    pass8(i, a)
            for i in range(6, TILES):
                pass4(i, 2)
                pass4(i, 3)
            drain(s, 0)
            drain(v, 1)
            store(0, 2)
            cast(v, "x2", 0, 256)
            cast(s, "x2", 256, 512)
            quantize("x2", 0, 256)
            drain(s, 2)
            drain(s, 3)
            store(2, 4)
            cast(v, "x3", 0, 128)
            quantize("x2", 256, 512)
            for i in range(4, 8):
                pass8(i, 0)
            quantize("x3", 0, 128)
            pass8(4, 1)
            cast(v, "x3", 128, 256)
            quantize("x3", 128, 256)
            pass8(5, 1)
            cast(s, "x4", 0, 128)
            cast(s, "x4", 128, 256)
            drain(v, 4)
            store(4, 5)
            quantize("x4", 0, 128)
            pass8(6, 1)
            drain(v, 5)
            store(5, 6)
            quantize("x4", 128, 256)
            pass8(7, 1)
            drain(s, 6)
            store(6, 7)
            drain(s, 7)
            store(7, 8)
